import numpy as np
import ml_dtypes


def mxq(x, axis, fmt="e4m3"):
    dtype, down = {"e4m3": (ml_dtypes.float8_e4m3fn, 7), "e5m2": (ml_dtypes.float8_e5m2, 14)}[fmt]
    v = np.moveaxis(np.asarray(x, np.float32).astype(ml_dtypes.bfloat16).astype(np.float64), axis, -1)
    blocks = v.reshape(v.shape[:-1] + (-1, 32))
    amax = np.abs(blocks).max(-1, keepdims=True)
    byte = np.maximum(np.where(amax > 0, np.frexp(amax)[1] - 1 + 127, 0) - down, 1)
    scale = np.exp2(byte - 127.0)
    codes = (blocks / scale).astype(np.float32).astype(dtype).astype(np.float64)
    return np.moveaxis((codes * scale).reshape(v.shape), -1, axis)


WIDE = False


def mx_kscale(k):
    if not WIDE:
        return np.ones(k)
    levels = np.array([10, -10, 5, -5, 0])
    if k % 512:
        return np.exp2(np.random.permutation(np.resize(levels, k // 32))).repeat(32)
    a = np.empty((k // 512, 16))
    for p in range(k // 512):
        a[p, :8] = np.random.permutation(np.resize(levels, 8))
        for g in range(8):
            far = levels[np.abs(levels - a[p, g]) >= 10]
            a[p, g + 8] = far[np.random.randint(len(far))]
    return np.exp2(a.ravel()).repeat(32)


BF16 = ml_dtypes.bfloat16


def bf(x):
    return np.asarray(x, np.float32).astype(BF16)


def f64(x):
    return np.asarray(x).astype(np.float64)


E2M1 = np.array([0.0, 0.5, 1.0, 1.5, 2.0, 3.0, 4.0, 6.0, -0.0, -0.5, -1.0, -1.5, -2.0, -3.0, -4.0, -6.0])


def pack_weight(w, fmt):
    k, n = w.shape
    w = f64(bf(w)).reshape(k // 32, 32, n)
    amax = np.abs(w).max(1)
    if fmt == "e4m3":
        byte = np.frexp(amax)[1] - 1 + 127 - 7
    else:
        mant, ex = np.frexp(amax / 6.0)
        byte = np.where(mant > 0.5, ex, ex - 1) + 127
    byte = np.clip(np.where(amax > 0, byte, 1), 1, 254)
    scaled = (w * np.exp2(127.0 - byte)[:, None, :]).reshape(k, n).astype(np.float32)
    by_word = np.ascontiguousarray(scaled.reshape(k // 512, 128, 4, n).transpose(0, 1, 3, 2))
    if fmt == "e4m3":
        words = by_word.astype(ml_dtypes.float8_e4m3fn).view(np.uint8)
    else:
        c = by_word.astype(ml_dtypes.float4_e2m1fn).view(np.uint8) & 0xF
        words = c[..., 0::2] | (c[..., 1::2] << 4)
    return np.ascontiguousarray(words), np.ascontiguousarray(byte.astype(np.uint8).reshape(k // 512, 16, n))


def unpack_weight(words, scales, fmt):
    g, p, n, _ = words.shape
    if fmt == "e4m3":
        vals = np.ascontiguousarray(words).view(ml_dtypes.float8_e4m3fn).astype(np.float64)
    else:
        nib = np.empty((g, p, n, 4), np.uint8)
        nib[..., 0::2] = words & 0xF
        nib[..., 1::2] = words >> 4
        vals = E2M1[nib]
    vals = vals * np.repeat(np.exp2(scales.astype(np.float64) - 127.0), 8, axis=1)[..., None]
    return vals.transpose(0, 1, 3, 2).reshape(g * 512, n)
def pack4(w):
    words, scales = pack_weight(w, "e2m1")
    return words.reshape(words.shape[0], 128, -1), scales


def unpack4(words, scales):
    return unpack_weight(words.reshape(words.shape[0], 128, -1, 2), scales, "e2m1")


S, KD, KI, N, H = 512, 1024, 2048, 2048, 512


def setup_inputs():
    sd, si, t = mx_kscale(KD), mx_kscale(KI), mx_kscale(N)
    imp_words, imp_scales = pack4(np.random.standard_normal((KI, N)) / np.sqrt(KI) / si[:, None])
    alloc_words, alloc_scales = pack4(np.random.standard_normal((N, H)) / np.sqrt(N) / t[:, None])
    return {"demand_dom": bf(np.random.standard_normal((S, KD)) * sd),
            "demand_imp": bf(np.random.standard_normal((S, KI)) * si),
            "req_dom": bf(np.random.standard_normal((KD, N)) / np.sqrt(KD) / sd[:, None]),
            "req_imp_words": imp_words,
            "req_imp_scales": imp_scales,
            "exports": bf(0.4 * np.random.standard_normal(N)),
            "intensity": bf(np.exp(0.5 * np.random.standard_normal(N)) * t),
            "alloc_words": alloc_words,
            "alloc_scales": alloc_scales,
            "direct": bf(0.4 * np.random.standard_normal(H))}


def reference(demand_dom, demand_imp, req_dom, req_imp_words, req_imp_scales,
              exports, intensity, alloc_words, alloc_scales, direct):
    dom = mxq(f64(demand_dom), 1, "e4m3") @ mxq(f64(req_dom), 0, "e4m3")
    imp = mxq(f64(demand_imp), 1, "e4m3") @ unpack4(req_imp_words, req_imp_scales)
    gross = dom + imp + f64(exports)
    emis = gross * f64(intensity)
    alloc = unpack4(alloc_words, alloc_scales)
    return (mxq(emis, 1, "e4m3") @ alloc) + f64(direct)

@@ -1,0 +1,385 @@
+from contextlib import ExitStack
+
+import concourse.mybir as mybir
+from concourse.masks import make_identity
+
+S, KD, KI, N, H = 512, 1024, 2048, 2048, 512
+FLOPS = 2 * S * ((KD + KI) * N + N * H)
+
+F32 = mybir.dt.float32
+BF16 = mybir.dt.bfloat16
+I32 = mybir.dt.int32
+U32 = mybir.dt.uint32
+U8 = mybir.dt.uint8
+FP8X4 = mybir.dt.float8_e4m3fn_x4
+FP4X4 = mybir.dt.float4_e2m1fn_x4
+IDENT = mybir.ActivationFunctionType.Identity
+ADD = mybir.AluOpType.add
+MULT = mybir.AluOpType.mult
+
+P = 128
+W = 512
+GI = KI // W
+GD = KD // W
+CH = N // W
+LAST = CH - 1
+WARM_A = 12
+WARM_B = 8
+
+
+def tile_leontief_footprint_allocation_s3_kernel(
+    tc, demand_dom, demand_imp, req_dom, req_imp_words, req_imp_scales,
+    exports, intensity, alloc_words, alloc_scales, direct, out,
+):
+    nc = tc.nc
+    with ExitStack() as ctx:
+        keep = ctx.enter_context(tc.tile_pool(name="keep", bufs=1))
+        rot = ctx.enter_context(tc.tile_pool(name="rot", bufs=4))
+        psum = ctx.enter_context(tc.psum_pool(name="psum", bufs=1))
+        ctx.enter_context(tc.manual_schedule())
+
+        def kept(name, shape, dtype):
+            return keep.tile(shape, dtype, name=name, align_bytes=64)
+
+        def bank(b, name):
+            return psum.tile([P, W], F32, name=name, tag="bank%d" % b)
+
+        ident = kept("ident", [P, P], F32)
+        warm_in = kept("warm_in", [P, W], BF16)
+        warm_codes = kept("warm_codes", [P, P], U32)
+        warm_scales = kept("warm_scales", [P, P], U8)
+        d_imp = [kept("d_imp%d" % g, [P, 4, W], BF16) for g in range(GI)]
+        d_dom = kept("d_dom", [P, 4, KD], BF16)
+        d_codes = [kept("d_codes%d" % g, [P, W], U32) for g in range(GI + GD)]
+        d_scales = [kept("d_scales%d" % g, [P, W], U8) for g in range(GI + GD)]
+        w0a = kept("w0a", [P, 1, 2 * W], U8)
+        w0b = kept("w0b", [P, GI - 1, 2 * W], U8)
+        w1 = kept("w1", [P, GI, 2 * W], U8)
+        w23 = kept("w23", [P, GI, 4 * W], U8)
+        w3 = [kept("w3_%d" % g, [P, 2 * W], U8) for g in range(GI)]
+        sc0 = kept("sc0", [P, GI, W], U8)
+        sc1 = kept("sc1", [P, GI, W], U8)
+        sc23 = kept("sc23", [P, GI, 2 * W], U8)
+        sc3 = kept("sc3", [P, GI, W], U8)
+        a_words = kept("a_words", [P, CH, 2 * H], U8)
+        a_scales = kept("a_scales", [P, CH, H], U8)
+        r_raw = {(c, g): kept("r_raw%d_%d" % (c, g), [P, 4, W], BF16) for c in range(CH) for g in range(GD)}
+        r_codes = {(c, g): kept("r_codes%d_%d" % (c, g), [P, W], U32) for c in range(CH) for g in range(GD)}
+        r_scales = {(c, g): kept("r_scales%d_%d" % (c, g), [P, W], U8) for c in range(CH) for g in range(GD)}
+        vec_rows = kept("vec_rows", [32, P], BF16)
+        vec_f32 = kept("vec_f32", [P, P], F32)
+        vec_cols = kept("vec_cols", [P, 32], F32)
+        bias_cols = kept("bias_cols", [P, 16], F32)
+        exp_last = kept("exp_last", [P, 4], BF16)
+        int_last = kept("int_last", [P, 4], BF16)
+        gain_last = kept("gain_last", [P, 4], F32)
+        bias_last = kept("bias_last", [P, 4], F32)
+        direct_rows = kept("direct_rows", [P, H], BF16)
+        emis = [kept("emis%d" % c, [P, 4, S], BF16) for c in range(CH)]
+        back = [kept("back%d" % c, [P, 4, S], BF16) for c in range(LAST)]
+        e_codes = [kept("e_codes%d" % c, [P, S], U32) for c in range(CH)]
+        e_scales = [kept("e_scales%d" % c, [P, S], U8) for c in range(CH)]
+        e_half = [kept("e_half%d" % h, [P, 2 * S], BF16) for h in range(2)]
+        result = [kept("result%d" % a, [P, H], F32) for a in range(4)]
+
+        words32 = req_imp_words.bitcast(I32).rearrange("g p n -> p g n")
+        dimp_v = demand_imp.rearrange("(r a) k -> r a k", a=4)
+        ddom_v = demand_dom.rearrange("(r a) k -> r a k", a=4)
+        park = out.bitcast(BF16).rearrange("a (b w) -> (a b) w", b=2)
+        out_v = out.rearrange("(r a) h -> r a h", a=4)
+
+        def load_scales(plane, src, col0, cols):
+            src32 = src.bitcast(I32)
+            for r in range(4):
+                nc.sync.dma_start(
+                    out=plane[r:P:32, :, :].bitcast(I32),
+                    in_=src32[:, r:16:4, col0 // 4:(col0 + cols) // 4].rearrange("g q n -> q g n"),
+                )
+
+        def load_words(dst, g0, g1, c0, c1):
+            nc.sync.dma_start(out=dst[:].bitcast(I32), in_=words32[:, g0:g1, c0 * W // 2:c1 * W // 2])
+
+        def load_req(c, g):
+            nc.sync.dma_start(
+                out=r_raw[c, g][:],
+                in_=req_dom[g * W:(g + 1) * W, c * W:(c + 1) * W].rearrange("(p j) n -> p j n", j=4),
+            )
+
+        def parked(c):
+            return park[(c % 2) * W:(c % 2 + 1) * W, :]
+
+        def store_emis(c, j0, j1):
+            nc.sync.dma_start(
+                out=parked(c).rearrange("(j p) w -> p j w", p=P)[:, j0:j1, :],
+                in_=emis[c][:, j0:j1, :],
+            )
+
+        def load_back(c):
+            nc.sync.dma_start(out=back[c][:], in_=parked(c).rearrange("(p t) w -> p t w", t=4))
+
+        def warm(dst, n):
+            for i in range(n):
+                nc.tensor.matmul_mx(
+                    out=dst[:, 0:P], lhsT=warm_codes[:].bitcast(FP8X4), lhsT_scale=warm_scales[:],
+                    rhs=warm_codes[:].bitcast(FP8X4), rhs_scale=warm_scales[:], start=(i == 0), stop=(i == n - 1),
+                )
+
+        grouped = {}
+
+        def turn_demand(g):
+            if g < GI:
+                words, first = d_imp[g][:].bitcast(F32), 0
+            else:
+                words, first = d_dom[:].bitcast(F32), (g - GI) * W // 2
+            grouped["d", g] = rot.tile([P, 4 * W], BF16, name="d_grouped", tag="grouped", align_bytes=64)
+            turned = []
+            for h in range(2):
+                xt = bank(4 + 2 * (g % 2) + h, "xt")
+                for a in range(2):
+                    for u in range(2):
+                        q = 2 * a + u
+                        nc.tensor.transpose(
+                            xt[:, q * P:(q + 1) * P], words[:, 2 * h + a, first + u:first + W // 2:2], ident[:],
+                        )
+                turned.append(xt)
+            for h in range(2):
+                nc.scalar.copy(
+                    out=grouped["d", g][:].bitcast(F32)[:, h * W:(h + 1) * W].rearrange("p (a r u) -> p a r u", a=2, u=2),
+                    in_=turned[h][:].rearrange("p (a u r) -> p a r u", a=2, u=2),
+                )
+
+        def quantise(key, codes, scales):
+            nc.vector.quantize_mx(out=codes[:].bitcast(FP8X4), scales=scales[:], in_=grouped[key][:])
+
+        def copy_on(engine, dst, src):
+            if engine == "scalar":
+                nc.scalar.copy(out=dst, in_=src)
+            else:
+                nc.vector.tensor_copy(out=dst, in_=src)
+
+        def interleave(engine, dst, src):
+            copy_on(
+                engine,
+                dst.rearrange("p (c i t) -> p c t i", i=4, t=4),
+                src.rearrange("p t (c i) -> p c t i", i=4),
+            )
+
+        def group_req(c, g, engine):
+            grouped["r", c, g] = rot.tile([P, 4 * W], BF16, name="r_grouped", tag="grouped", align_bytes=64)
+            dst = grouped["r", c, g][:]
+            if c < LAST:
+                interleave(engine, dst, r_raw[c, g][:])
+            else:
+                copy_on(
+                    engine,
+                    dst.rearrange("p (t m j) -> p t m j", t=4, j=4),
+                    r_raw[c, g][:].rearrange("p j (m t) -> p t m j", t=4),
+                )
+
+        def quantise_req(c, g):
+            quantise(("r", c, g), r_codes[c, g], r_scales[c, g])
+
+        def group_emis(c):
+            grouped["e", c] = rot.tile([P, 4 * S], BF16, name="e_grouped", tag="grouped", align_bytes=64)
+            interleave("vector", grouped["e", c][:], back[c][:])
+
+        def quantise_emis(c):
+            quantise(("e", c), e_codes[c], e_scales[c])
+
+        def imp_operand(c, g, j):
+            if c == 0:
+                wt = w0a[:, 0, :] if g == 0 else w0b[:, g - 1, :]
+                st = sc0[:, g, :]
+            elif c == 1:
+                wt, st = w1[:, g, :], sc1[:, g, :]
+            elif c == 2:
+                wt, st = w23[:, g, 0:2 * W], sc23[:, g, 0:W]
+            else:
+                wt, st = w3[g][:], sc3[:, g, :]
+            return wt[:, 2 * j * P:2 * (j + 1) * P].bitcast(FP4X4), st[:, j * P:(j + 1) * P]
+
+        gross = {}
+
+        def gross_pass(c, g, j):
+            if g == 0:
+                gross[c, j] = bank(4 * (c % 2) + j, "gross")
+            if g < GI:
+                lhs, lhs_scale = imp_operand(c, g, j)
+            else:
+                cols = slice(j * P, (j + 1) * P)
+                lhs, lhs_scale = r_codes[c, g - GI][:, cols].bitcast(FP8X4), r_scales[c, g - GI][:, cols]
+            nc.tensor.matmul_mx(
+                out=gross[c, j][:], lhsT=lhs, lhsT_scale=lhs_scale,
+                rhs=d_codes[g][:].bitcast(FP8X4), rhs_scale=d_scales[g][:],
+                start=(g == 0), stop=(g == GI + GD - 1),
+            )
+
+        def imp_passes(c):
+            for g in range(GI):
+                for j in range(4):
+                    gross_pass(c, g, j)
+
+        def emit(c, j):
+            if c < LAST:
+                col = 4 * c + j
+                gain, bias = vec_cols[:, 16 + col:17 + col], bias_cols[:, col:col + 1]
+            else:
+                gain, bias = gain_last[:, j:j + 1], bias_last[:, j:j + 1]
+            nc.scalar.activation(out=emis[c][:, j, :], in_=gross[c, j][:], func=IDENT, bias=bias, scale=gain)
+
+        def dom_passes(c):
+            for j in range(4):
+                for g in range(GI, GI + GD):
+                    gross_pass(c, g, j)
+                emit(c, j)
+
+        acc = {}
+
+        def alloc_pass(c, a):
+            if c == 0:
+                acc[a] = bank(a, "acc")
+            cols = slice(a * P, (a + 1) * P)
+            nc.tensor.matmul_mx(
+                out=acc[a][:], lhsT=e_codes[c][:, cols].bitcast(FP8X4), lhsT_scale=e_scales[c][:, cols],
+                rhs=a_words[:, c, :].bitcast(FP4X4), rhs_scale=a_scales[:, c, :],
+                start=(c == 0), stop=(c == LAST),
+            )
+
+        def finish(a):
+            nc.vector.tensor_tensor(out=result[a][:], in0=acc[a][:], in1=direct_rows[:], op=ADD)
+            nc.sync.dma_start(out=out_v[:, a, :], in_=result[a][:])
+
+        def zero(plane):
+            nc.vector.memset(plane[:].bitcast(I32), 0)
+
+        nc.sync.dma_start(out=d_imp[0][:], in_=dimp_v[:, :, 0:W])
+        zero(warm_in)
+        zero(sc0)
+        nc.vector.quantize_mx(out=warm_codes[:].bitcast(FP8X4), scales=warm_scales[:], in_=warm_in[:])
+        zero(sc1)
+        zero(sc23)
+        zero(a_scales)
+        make_identity(nc, ident[:])
+        nc.scalar.activation(out=vec_f32[:], in_=ident[:], func=IDENT, scale=0.0)
+
+        load_scales(sc0, req_imp_scales, 0, W)
+        load_words(w0a, 0, 1, 0, 1)
+        nc.sync.dma_start(out=d_imp[1][:], in_=dimp_v[:, :, W:2 * W])
+        load_words(w0b, 1, GI, 0, 1)
+        for g in range(2, GI):
+            nc.sync.dma_start(out=d_imp[g][:], in_=dimp_v[:, :, g * W:(g + 1) * W])
+        nc.sync.dma_start(out=vec_rows[0:16, :], in_=exports.rearrange("(j p) -> j p", p=P))
+        nc.sync.dma_start(out=vec_rows[16:32, :], in_=intensity.rearrange("(j p) -> j p", p=P))
+        nc.sync.dma_start(out=d_dom[:], in_=ddom_v)
+        load_req(0, 0)
+        load_req(0, 1)
+        load_scales(sc1, req_imp_scales, W, W)
+        load_words(w1, 0, GI, 1, 2)
+        load_req(1, 0)
+        load_req(1, 1)
+        load_scales(sc23, req_imp_scales, 2 * W, 2 * W)
+        load_words(w23, 0, GI, 2, 4)
+        load_req(2, 0)
+        load_req(2, 1)
+
+        warm_bank = bank(3, "warm_bank")
+        warm(warm_bank, WARM_A)
+        turn_demand(0)
+        warm(warm_bank, WARM_B)
+        quantise(("d", 0), d_codes[0], d_scales[0])
+        for g in range(1, GI + GD):
+            turn_demand(g)
+            if g == GI + GD - 1:
+                vec_bank = bank(4, "vec_bank")
+                nc.tensor.transpose(vec_bank[:, 0:P], vec_f32[:], ident[:])
+                nc.scalar.copy(out=vec_cols[:], in_=vec_bank[:, 0:32])
+            for j in range(4):
+                gross_pass(0, g - 1, j)
+            quantise(("d", g), d_codes[g], d_scales[g])
+            if g == GI - 1:
+                nc.vector.tensor_copy(out=vec_f32[0:32, :], in_=vec_rows[:])
+                group_req(0, 0, "vector")
+            if g == GI:
+                quantise_req(0, 0)
+                group_req(0, 1, "vector")
+        nc.vector.tensor_tensor(out=bias_cols[:], in0=vec_cols[:, 0:16], in1=vec_cols[:, 16:32], op=MULT)
+        quantise_req(0, 1)
+        for j in range(4):
+            gross_pass(0, GI + GD - 1, j)
+            emit(0, j)
+        store_emis(0, 0, 4)
+        load_req(3, 0)
+        load_req(3, 1)
+        load_back(0)
+
+        imp_passes(1)
+        group_req(1, 0, "vector")
+        group_req(1, 1, "vector")
+        quantise_req(1, 0)
+        quantise_req(1, 1)
+        dom_passes(1)
+        store_emis(1, 0, 4)
+        load_scales(a_scales, alloc_scales, 0, H)
+        nc.sync.dma_start(out=a_words[:].bitcast(I32), in_=alloc_words.bitcast(I32).rearrange("g p n -> p g n"))
+        load_back(1)
+        nc.sync.dma_start(out=exp_last[:], in_=exports[LAST * W:].rearrange("(p t) -> p t", t=4))
+        nc.sync.dma_start(out=int_last[:], in_=intensity[LAST * W:].rearrange("(p t) -> p t", t=4))
+        nc.sync.dma_start(out=direct_rows[:], in_=direct.partition_broadcast(P))
+
+        imp_passes(2)
+
+        def sort_words(g):
+            nc.vector.tensor_copy(
+                out=w3[g][:].rearrange("p (t m b) -> p t m b", t=4, b=2),
+                in_=w23[:, g, 2 * W:4 * W].rearrange("p (m t b) -> p t m b", t=4, b=2),
+            )
+
+        sort_words(0)
+        sort_words(1)
+        group_req(2, 0, "vector")
+        group_req(2, 1, "scalar")
+        sort_words(2)
+        quantise_req(2, 0)
+        sort_words(3)
+        quantise_req(2, 1)
+        nc.vector.tensor_copy(
+            out=sc3[:].rearrange("p g (t m) -> p g t m", t=4),
+            in_=sc23[:, :, W:2 * W].rearrange("p g (m t) -> p g t m", t=4),
+        )
+        dom_passes(2)
+        store_emis(2, 0, 2)
+        store_emis(2, 2, 4)
+        load_back(2)
+
+        imp_passes(3)
+        group_req(3, 0, "vector")
+        group_emis(0)
+        quantise_req(3, 0)
+        quantise_emis(0)
+        group_req(3, 1, "scalar")
+        group_emis(1)
+        nc.vector.tensor_copy(out=gain_last[:], in_=int_last[:])
+        nc.vector.tensor_tensor(out=bias_last[:], in0=exp_last[:], in1=int_last[:], op=MULT)
+        quantise_emis(1)
+        quantise_req(3, 1)
+        dom_passes(3)
+        group_emis(2)
+        quantise_emis(2)
+
+        half = S // 2
+        interleave("vector", e_half[0][:], emis[LAST][:, :, 0:half])
+        interleave("scalar", e_half[1][:], emis[LAST][:, :, half:S])
+        for h in range(2):
+            cols = slice(h * half, (h + 1) * half)
+            nc.vector.quantize_mx(
+                out=e_codes[LAST][:, cols].bitcast(FP8X4), scales=e_scales[LAST][:, cols], in_=e_half[h][:],
+            )
+        for c in range(2):
+            for a in range(4):
+                alloc_pass(c, a)
+        for pair in ((0, 1), (2, 3)):
+            for c in (2, 3):
+                for a in pair:
+                    alloc_pass(c, a)
+            for a in pair:
+                finish(a)

@@ -23,6 +23,8 @@ GI = KI // W
 GD = KD // W
 CH = N // W
 LAST = CH - 1
+SORTED = (0, LAST)
+PARKED = (1, 2)
 WARM_A = 12
 WARM_B = 8
 
@@ -53,14 +55,15 @@ def tile_leontief_footprint_allocation_s3_kernel(
         d_codes = [kept("d_codes%d" % g, [P, W], U32) for g in range(GI + GD)]
         d_scales = [kept("d_scales%d" % g, [P, W], U8) for g in range(GI + GD)]
         w0a = kept("w0a", [P, 1, 2 * W], U8)
-        w0b = kept("w0b", [P, GI - 1, 2 * W], U8)
+        w0b = kept("w0b", [P, 1, 2 * W], U8)
+        w0c = kept("w0c", [P, 2, 2 * W], U8)
         w1 = kept("w1", [P, GI, 2 * W], U8)
         w23 = kept("w23", [P, GI, 4 * W], U8)
-        w3 = [kept("w3_%d" % g, [P, 2 * W], U8) for g in range(GI)]
+        w_sorted = {(c, g): kept("w_sorted%d_%d" % (c, g), [P, 2 * W], U8) for c in SORTED for g in range(GI)}
+        sc_sorted = {(c, g): kept("sc_sorted%d_%d" % (c, g), [P, W], U8) for c in SORTED for g in range(GI)}
         sc0 = kept("sc0", [P, GI, W], U8)
         sc1 = kept("sc1", [P, GI, W], U8)
         sc23 = kept("sc23", [P, GI, 2 * W], U8)
-        sc3 = kept("sc3", [P, GI, W], U8)
         a_words = kept("a_words", [P, CH, 2 * H], U8)
         a_scales = kept("a_scales", [P, CH, H], U8)
         r_raw = {(c, g): kept("r_raw%d_%d" % (c, g), [P, 4, W], BF16) for c in range(CH) for g in range(GD)}
@@ -70,13 +73,13 @@ def tile_leontief_footprint_allocation_s3_kernel(
         vec_f32 = kept("vec_f32", [P, P], F32)
         vec_cols = kept("vec_cols", [P, 32], F32)
         bias_cols = kept("bias_cols", [P, 16], F32)
-        exp_last = kept("exp_last", [P, 4], BF16)
-        int_last = kept("int_last", [P, 4], BF16)
-        gain_last = kept("gain_last", [P, 4], F32)
-        bias_last = kept("bias_last", [P, 4], F32)
+        exp_sorted = kept("exp_sorted", [P, 2, 4], BF16)
+        int_sorted = kept("int_sorted", [P, 2, 4], BF16)
+        gain_sorted = kept("gain_sorted", [P, 2, 4], F32)
+        bias_sorted = kept("bias_sorted", [P, 2, 4], F32)
         direct_rows = kept("direct_rows", [P, H], BF16)
         emis = [kept("emis%d" % c, [P, 4, S], BF16) for c in range(CH)]
-        back = [kept("back%d" % c, [P, 4, S], BF16) for c in range(LAST)]
+        back = {c: kept("back%d" % c, [P, 4, S], BF16) for c in PARKED}
         e_codes = [kept("e_codes%d" % c, [P, S], U32) for c in range(CH)]
         e_scales = [kept("e_scales%d" % c, [P, S], U8) for c in range(CH)]
         e_half = [kept("e_half%d" % h, [P, 2 * S], BF16) for h in range(2)]
@@ -167,7 +170,7 @@ def tile_leontief_footprint_allocation_s3_kernel(
         def group_req(c, g, engine):
             grouped["r", c, g] = rot.tile([P, 4 * W], BF16, name="r_grouped", tag="grouped", align_bytes=64)
             dst = grouped["r", c, g][:]
-            if c < LAST:
+            if c in PARKED:
                 interleave(engine, dst, r_raw[c, g][:])
             else:
                 copy_on(
@@ -179,23 +182,41 @@ def tile_leontief_footprint_allocation_s3_kernel(
         def quantise_req(c, g):
             quantise(("r", c, g), r_codes[c, g], r_scales[c, g])
 
-        def group_emis(c):
+        def group_emis(c, engine):
             grouped["e", c] = rot.tile([P, 4 * S], BF16, name="e_grouped", tag="grouped", align_bytes=64)
-            interleave("vector", grouped["e", c][:], back[c][:])
+            interleave(engine, grouped["e", c][:], back[c][:] if c in PARKED else emis[c][:])
 
         def quantise_emis(c):
             quantise(("e", c), e_codes[c], e_scales[c])
 
-        def imp_operand(c, g, j):
+        def loaded_imp(c, g):
             if c == 0:
-                wt = w0a[:, 0, :] if g == 0 else w0b[:, g - 1, :]
-                st = sc0[:, g, :]
-            elif c == 1:
-                wt, st = w1[:, g, :], sc1[:, g, :]
-            elif c == 2:
-                wt, st = w23[:, g, 0:2 * W], sc23[:, g, 0:W]
+                return (w0a[:, 0, :], w0b[:, 0, :], w0c[:, 0, :], w0c[:, 1, :])[g], sc0[:, g, :]
+            if c == 1:
+                return w1[:, g, :], sc1[:, g, :]
+            return w23[:, g, (c - 2) * 2 * W:(c - 1) * 2 * W], sc23[:, g, (c - 2) * W:(c - 1) * W]
+
+        def sort_words(c, g):
+            nc.vector.tensor_copy(
+                out=w_sorted[c, g][:].rearrange("p (t m b) -> p t m b", t=4, b=2),
+                in_=loaded_imp(c, g)[0].rearrange("p (m t b) -> p t m b", t=4, b=2),
+            )
+
+        def sort_scales(c, g):
+            nc.vector.tensor_copy(
+                out=sc_sorted[c, g][:].rearrange("p (t m) -> p t m", t=4),
+                in_=loaded_imp(c, g)[1].rearrange("p (m t) -> p t m", t=4),
+            )
+
+        def sort_imp(c, g):
+            sort_words(c, g)
+            sort_scales(c, g)
+
+        def imp_operand(c, g, j):
+            if c in SORTED:
+                wt, st = w_sorted[c, g][:], sc_sorted[c, g][:]
             else:
-                wt, st = w3[g][:], sc3[:, g, :]
+                wt, st = loaded_imp(c, g)
             return wt[:, 2 * j * P:2 * (j + 1) * P].bitcast(FP4X4), st[:, j * P:(j + 1) * P]
 
         gross = {}
@@ -220,11 +241,11 @@ def tile_leontief_footprint_allocation_s3_kernel(
                     gross_pass(c, g, j)
 
         def emit(c, j):
-            if c < LAST:
+            if c in PARKED:
                 col = 4 * c + j
                 gain, bias = vec_cols[:, 16 + col:17 + col], bias_cols[:, col:col + 1]
             else:
-                gain, bias = gain_last[:, j:j + 1], bias_last[:, j:j + 1]
+                gain, bias = gain_sorted[:, c // LAST, j:j + 1], bias_sorted[:, c // LAST, j:j + 1]
             nc.scalar.activation(out=emis[c][:, j, :], in_=gross[c, j][:], func=IDENT, bias=bias, scale=gain)
 
         def dom_passes(c):
@@ -262,17 +283,20 @@ def tile_leontief_footprint_allocation_s3_kernel(
         make_identity(nc, ident[:])
         nc.scalar.activation(out=vec_f32[:], in_=ident[:], func=IDENT, scale=0.0)
 
-        load_scales(sc0, req_imp_scales, 0, W)
         load_words(w0a, 0, 1, 0, 1)
         nc.sync.dma_start(out=d_imp[1][:], in_=dimp_v[:, :, W:2 * W])
-        load_words(w0b, 1, GI, 0, 1)
-        for g in range(2, GI):
-            nc.sync.dma_start(out=d_imp[g][:], in_=dimp_v[:, :, g * W:(g + 1) * W])
+        load_scales(sc0, req_imp_scales, 0, W)
+        load_words(w0b, 1, 2, 0, 1)
+        nc.sync.dma_start(out=d_imp[2][:], in_=dimp_v[:, :, 2 * W:3 * W])
+        load_words(w0c, 2, GI, 0, 1)
+        nc.sync.dma_start(out=d_imp[3][:], in_=dimp_v[:, :, 3 * W:4 * W])
+        nc.sync.dma_start(out=d_dom[:], in_=ddom_v)
         nc.sync.dma_start(out=vec_rows[0:16, :], in_=exports.rearrange("(j p) -> j p", p=P))
         nc.sync.dma_start(out=vec_rows[16:32, :], in_=intensity.rearrange("(j p) -> j p", p=P))
-        nc.sync.dma_start(out=d_dom[:], in_=ddom_v)
         load_req(0, 0)
         load_req(0, 1)
+        nc.sync.dma_start(out=exp_sorted[:], in_=exports.rearrange("(c p t) -> p c t", p=P, t=4)[:, 0:CH:LAST, :])
+        nc.sync.dma_start(out=int_sorted[:], in_=intensity.rearrange("(c p t) -> p c t", p=P, t=4)[:, 0:CH:LAST, :])
         load_scales(sc1, req_imp_scales, W, W)
         load_words(w1, 0, GI, 1, 2)
         load_req(1, 0)
@@ -281,89 +305,93 @@ def tile_leontief_footprint_allocation_s3_kernel(
         load_words(w23, 0, GI, 2, 4)
         load_req(2, 0)
         load_req(2, 1)
+        load_req(3, 0)
+        load_req(3, 1)
+
+        def quantise_demand(g):
+            quantise(("d", g), d_codes[g], d_scales[g])
+
+        def head_pass(g):
+            for j in range(4):
+                gross_pass(0, g, j)
 
         warm_bank = bank(3, "warm_bank")
         warm(warm_bank, WARM_A)
         turn_demand(0)
         warm(warm_bank, WARM_B)
-        quantise(("d", 0), d_codes[0], d_scales[0])
-        for g in range(1, GI + GD):
-            turn_demand(g)
-            if g == GI + GD - 1:
-                vec_bank = bank(4, "vec_bank")
-                nc.tensor.transpose(vec_bank[:, 0:P], vec_f32[:], ident[:])
-                nc.scalar.copy(out=vec_cols[:], in_=vec_bank[:, 0:32])
-            for j in range(4):
-                gross_pass(0, g - 1, j)
-            quantise(("d", g), d_codes[g], d_scales[g])
-            if g == GI - 1:
-                nc.vector.tensor_copy(out=vec_f32[0:32, :], in_=vec_rows[:])
-                group_req(0, 0, "vector")
-            if g == GI:
-                quantise_req(0, 0)
-                group_req(0, 1, "vector")
-        nc.vector.tensor_tensor(out=bias_cols[:], in0=vec_cols[:, 0:16], in1=vec_cols[:, 16:32], op=MULT)
+        sort_words(0, 0)
+        quantise_demand(0)
+        sort_scales(0, 0)
+        turn_demand(1)
+        head_pass(0)
+        sort_imp(0, 1)
+        quantise_demand(1)
+        turn_demand(2)
+        head_pass(1)
+        sort_imp(0, 2)
+        quantise_demand(2)
+        sort_imp(0, 3)
+        turn_demand(3)
+        head_pass(2)
+        quantise_demand(3)
+        nc.vector.tensor_copy(out=vec_f32[0:32, :], in_=vec_rows[:])
+        turn_demand(4)
+        head_pass(3)
+        group_req(0, 0, "vector")
+        quantise_demand(4)
+        quantise_req(0, 0)
+        turn_demand(5)
+        vec_bank = bank(4, "vec_bank")
+        nc.tensor.transpose(vec_bank[:, 0:P], vec_f32[:], ident[:])
+        nc.scalar.copy(out=vec_cols[:], in_=vec_bank[:, 0:32])
+        head_pass(4)
+        group_req(0, 1, "vector")
+        quantise_demand(5)
         quantise_req(0, 1)
+        nc.vector.tensor_copy(out=gain_sorted[:], in_=int_sorted[:])
+        nc.vector.tensor_tensor(out=bias_sorted[:], in0=exp_sorted[:], in1=int_sorted[:], op=MULT)
+        nc.vector.tensor_tensor(out=bias_cols[:], in0=vec_cols[:, 0:16], in1=vec_cols[:, 16:32], op=MULT)
         for j in range(4):
             gross_pass(0, GI + GD - 1, j)
             emit(0, j)
-        store_emis(0, 0, 4)
-        load_req(3, 0)
-        load_req(3, 1)
-        load_back(0)
 
         imp_passes(1)
+        group_emis(0, "scalar")
         group_req(1, 0, "vector")
         group_req(1, 1, "vector")
         quantise_req(1, 0)
         quantise_req(1, 1)
+        quantise_emis(0)
         dom_passes(1)
         store_emis(1, 0, 4)
         load_scales(a_scales, alloc_scales, 0, H)
         nc.sync.dma_start(out=a_words[:].bitcast(I32), in_=alloc_words.bitcast(I32).rearrange("g p n -> p g n"))
         load_back(1)
-        nc.sync.dma_start(out=exp_last[:], in_=exports[LAST * W:].rearrange("(p t) -> p t", t=4))
-        nc.sync.dma_start(out=int_last[:], in_=intensity[LAST * W:].rearrange("(p t) -> p t", t=4))
-        nc.sync.dma_start(out=direct_rows[:], in_=direct.partition_broadcast(P))
 
         imp_passes(2)
-
-        def sort_words(g):
-            nc.vector.tensor_copy(
-                out=w3[g][:].rearrange("p (t m b) -> p t m b", t=4, b=2),
-                in_=w23[:, g, 2 * W:4 * W].rearrange("p (m t b) -> p t m b", t=4, b=2),
-            )
-
-        sort_words(0)
-        sort_words(1)
+        sort_imp(3, 0)
+        sort_imp(3, 1)
         group_req(2, 0, "vector")
         group_req(2, 1, "scalar")
-        sort_words(2)
+        sort_imp(3, 2)
         quantise_req(2, 0)
-        sort_words(3)
         quantise_req(2, 1)
-        nc.vector.tensor_copy(
-            out=sc3[:].rearrange("p g (t m) -> p g t m", t=4),
-            in_=sc23[:, :, W:2 * W].rearrange("p g (m t) -> p g t m", t=4),
-        )
+        sort_imp(3, 3)
         dom_passes(2)
         store_emis(2, 0, 2)
         store_emis(2, 2, 4)
         load_back(2)
+        nc.sync.dma_start(out=direct_rows[:], in_=direct.partition_broadcast(P))
 
         imp_passes(3)
         group_req(3, 0, "vector")
-        group_emis(0)
-        quantise_req(3, 0)
-        quantise_emis(0)
         group_req(3, 1, "scalar")
-        group_emis(1)
-        nc.vector.tensor_copy(out=gain_last[:], in_=int_last[:])
-        nc.vector.tensor_tensor(out=bias_last[:], in0=exp_last[:], in1=int_last[:], op=MULT)
+        group_emis(1, "vector")
+        quantise_req(3, 0)
         quantise_emis(1)
         quantise_req(3, 1)
         dom_passes(3)
-        group_emis(2)
+        group_emis(2, "vector")
         quantise_emis(2)
 
         half = S // 2

@@ -21,12 +21,14 @@ P = 128
 W = 512
 GI = KI // W
 GD = KD // W
+G = GI + GD
 CH = N // W
 LAST = CH - 1
-SORTED = (0, LAST)
-PARKED = (1, 2)
-WARM_A = 12
-WARM_B = 8
+PARKED = (0, 1)
+SORTED = (2, 3)
+WARM_A = 16
+WARM_B = 6
+WARM_C = 2
 
 
 def tile_leontief_footprint_allocation_s3_kernel(
@@ -36,7 +38,7 @@ def tile_leontief_footprint_allocation_s3_kernel(
     nc = tc.nc
     with ExitStack() as ctx:
         keep = ctx.enter_context(tc.tile_pool(name="keep", bufs=1))
-        rot = ctx.enter_context(tc.tile_pool(name="rot", bufs=4))
+        rot = ctx.enter_context(tc.tile_pool(name="rot", bufs=5))
         psum = ctx.enter_context(tc.psum_pool(name="psum", bufs=1))
         ctx.enter_context(tc.manual_schedule())
 
@@ -50,29 +52,32 @@ def tile_leontief_footprint_allocation_s3_kernel(
         warm_in = kept("warm_in", [P, W], BF16)
         warm_codes = kept("warm_codes", [P, P], U32)
         warm_scales = kept("warm_scales", [P, P], U8)
-        d_imp = [kept("d_imp%d" % g, [P, 4, W], BF16) for g in range(GI)]
-        d_dom = kept("d_dom", [P, 4, KD], BF16)
-        d_codes = [kept("d_codes%d" % g, [P, W], U32) for g in range(GI + GD)]
-        d_scales = [kept("d_scales%d" % g, [P, W], U8) for g in range(GI + GD)]
+        d_first = [kept("d_first%d" % h, [P, 2, W], BF16) for h in range(2)]
+        d_raw = {g: kept("d_raw%d" % g, [P, 4, W], BF16) for g in range(1, G)}
+        d_codes = [kept("d_codes%d" % g, [P, W], U32) for g in range(G)]
+        d_scales = [kept("d_scales%d" % g, [P, W], U8) for g in range(G)]
         w0a = kept("w0a", [P, 1, 2 * W], U8)
         w0b = kept("w0b", [P, 1, 2 * W], U8)
         w0c = kept("w0c", [P, 2, 2 * W], U8)
-        w1 = kept("w1", [P, GI, 2 * W], U8)
-        w23 = kept("w23", [P, GI, 4 * W], U8)
+        w12 = [kept("w12_%d" % h, [P, 2, 4 * W], U8) for h in range(2)]
+        w3 = kept("w3", [P, GI, 2 * W], U8)
+        sc0 = kept("sc0", [P, GI, W], U8)
+        sc12 = kept("sc12", [P, GI, 2 * W], U8)
+        sc3 = kept("sc3", [P, GI, W], U8)
         w_sorted = {(c, g): kept("w_sorted%d_%d" % (c, g), [P, 2 * W], U8) for c in SORTED for g in range(GI)}
         sc_sorted = {(c, g): kept("sc_sorted%d_%d" % (c, g), [P, W], U8) for c in SORTED for g in range(GI)}
-        sc0 = kept("sc0", [P, GI, W], U8)
-        sc1 = kept("sc1", [P, GI, W], U8)
-        sc23 = kept("sc23", [P, GI, 2 * W], U8)
         a_words = kept("a_words", [P, CH, 2 * H], U8)
         a_scales = kept("a_scales", [P, CH, H], U8)
-        r_raw = {(c, g): kept("r_raw%d_%d" % (c, g), [P, 4, W], BF16) for c in range(CH) for g in range(GD)}
+        r_raw = {
+            (c, g): kept("r_raw%d_%d" % (c, g), [P, 4, n * W], BF16)
+            for c, n in ((0, 1), (1, 1), (2, 2)) for g in range(GD)
+        }
         r_codes = {(c, g): kept("r_codes%d_%d" % (c, g), [P, W], U32) for c in range(CH) for g in range(GD)}
         r_scales = {(c, g): kept("r_scales%d_%d" % (c, g), [P, W], U8) for c in range(CH) for g in range(GD)}
-        vec_rows = kept("vec_rows", [32, P], BF16)
+        vec_rows = kept("vec_rows", [16, P], BF16)
         vec_f32 = kept("vec_f32", [P, P], F32)
-        vec_cols = kept("vec_cols", [P, 32], F32)
-        bias_cols = kept("bias_cols", [P, 16], F32)
+        vec_cols = kept("vec_cols", [P, 16], F32)
+        bias_cols = kept("bias_cols", [P, 8], F32)
         exp_sorted = kept("exp_sorted", [P, 2, 4], BF16)
         int_sorted = kept("int_sorted", [P, 2, 4], BF16)
         gain_sorted = kept("gain_sorted", [P, 2, 4], F32)
@@ -82,7 +87,7 @@ def tile_leontief_footprint_allocation_s3_kernel(
         back = {c: kept("back%d" % c, [P, 4, S], BF16) for c in PARKED}
         e_codes = [kept("e_codes%d" % c, [P, S], U32) for c in range(CH)]
         e_scales = [kept("e_scales%d" % c, [P, S], U8) for c in range(CH)]
-        e_half = [kept("e_half%d" % h, [P, 2 * S], BF16) for h in range(2)]
+        e_quarter = [kept("e_quarter%d" % a, [P, 4 * P], BF16) for a in range(4)]
         result = [kept("result%d" % a, [P, H], F32) for a in range(4)]
 
         words32 = req_imp_words.bitcast(I32).rearrange("g p n -> p g n")
@@ -102,20 +107,36 @@ def tile_leontief_footprint_allocation_s3_kernel(
         def load_words(dst, g0, g1, c0, c1):
             nc.sync.dma_start(out=dst[:].bitcast(I32), in_=words32[:, g0:g1, c0 * W // 2:c1 * W // 2])
 
-        def load_req(c, g):
+        def load_demand(g):
+            if g < GI:
+                src = dimp_v[:, :, g * W:(g + 1) * W]
+            else:
+                src = ddom_v[:, :, (g - GI) * W:(g - GI + 1) * W]
+            nc.sync.dma_start(out=d_raw[g][:], in_=src)
+
+        def load_req(c0, c1, g):
             nc.sync.dma_start(
-                out=r_raw[c, g][:],
-                in_=req_dom[g * W:(g + 1) * W, c * W:(c + 1) * W].rearrange("(p j) n -> p j n", j=4),
+                out=r_raw[c0, g][:],
+                in_=req_dom[g * W:(g + 1) * W, c0 * W:c1 * W].rearrange("(p j) n -> p j n", j=4),
             )
+
+        def loaded_req(c, g):
+            if c == LAST:
+                return r_raw[2, g][:, :, W:2 * W]
+            return r_raw[c, g][:, :, 0:W]
+
+        def loaded_imp(c, g):
+            if c == 0:
+                return (w0a[:, 0, :], w0b[:, 0, :], w0c[:, 0, :], w0c[:, 1, :])[g], sc0[:, g, :]
+            if c == LAST:
+                return w3[:, g, :], sc3[:, g, :]
+            return w12[g // 2][:, g % 2, (c - 1) * 2 * W:c * 2 * W], sc12[:, g, (c - 1) * W:c * W]
 
         def parked(c):
-            return park[(c % 2) * W:(c % 2 + 1) * W, :]
+            return park[c * W:(c + 1) * W, :]
 
-        def store_emis(c, j0, j1):
-            nc.sync.dma_start(
-                out=parked(c).rearrange("(j p) w -> p j w", p=P)[:, j0:j1, :],
-                in_=emis[c][:, j0:j1, :],
-            )
+        def store_emis(c):
+            nc.sync.dma_start(out=parked(c).rearrange("(j p) w -> p j w", p=P), in_=emis[c][:])
 
         def load_back(c):
             nc.sync.dma_start(out=back[c][:], in_=parked(c).rearrange("(p t) w -> p t w", t=4))
@@ -128,31 +149,47 @@ def tile_leontief_footprint_allocation_s3_kernel(
                 )
 
         grouped = {}
+        presorted = {}
+
+        def presort(g, h):
+            if g == 0:
+                words = d_first[h][:].bitcast(F32)
+            else:
+                words = d_raw[g][:].bitcast(F32)[:, 2 * h:2 * h + 2, :]
+            presorted[g, h] = rot.tile([P, 2, 2, P], F32, name="presorted", tag="presorted", bufs=4, align_bytes=64)
+            nc.vector.tensor_copy(
+                out=presorted[g, h][:].rearrange("p u a (o i) -> p (a o) u i", i=4),
+                in_=words.rearrange("p a (o i u) -> p (a o) u i", i=4, u=2),
+            )
+
+        def presort_demand(g):
+            for h in range(2):
+                presort(g, h)
+
+        def turn_half(g, h):
+            if h == 0:
+                grouped["d", g] = rot.tile([P, 4 * W], BF16, name="d_grouped", tag="grouped", align_bytes=64)
+            xt = bank(4 + 2 * (g % 2) + h, "xt")
+            for a in range(2):
+                for u in range(2):
+                    q = 2 * a + u
+                    nc.tensor.transpose(xt[:, q * P:(q + 1) * P], presorted[g, h][:, u, a, :], ident[:])
+            nc.scalar.copy(
+                out=grouped["d", g][:].bitcast(F32)[:, h * W:(h + 1) * W].rearrange("p (a r u) -> p a r u", a=2, u=2),
+                in_=xt[:].rearrange("p (a u r) -> p a r u", a=2, u=2),
+            )
 
         def turn_demand(g):
-            if g < GI:
-                words, first = d_imp[g][:].bitcast(F32), 0
-            else:
-                words, first = d_dom[:].bitcast(F32), (g - GI) * W // 2
-            grouped["d", g] = rot.tile([P, 4 * W], BF16, name="d_grouped", tag="grouped", align_bytes=64)
-            turned = []
             for h in range(2):
-                xt = bank(4 + 2 * (g % 2) + h, "xt")
-                for a in range(2):
-                    for u in range(2):
-                        q = 2 * a + u
-                        nc.tensor.transpose(
-                            xt[:, q * P:(q + 1) * P], words[:, 2 * h + a, first + u:first + W // 2:2], ident[:],
-                        )
-                turned.append(xt)
-            for h in range(2):
-                nc.scalar.copy(
-                    out=grouped["d", g][:].bitcast(F32)[:, h * W:(h + 1) * W].rearrange("p (a r u) -> p a r u", a=2, u=2),
-                    in_=turned[h][:].rearrange("p (a u r) -> p a r u", a=2, u=2),
-                )
+                turn_half(g, h)
 
-        def quantise(key, codes, scales):
-            nc.vector.quantize_mx(out=codes[:].bitcast(FP8X4), scales=scales[:], in_=grouped[key][:])
+        def quantise(codes, scales, values):
+            nc.vector.quantize_mx(out=codes.bitcast(FP8X4), scales=scales, in_=values)
+
+        def quantise_demand(g):
+            for h in range(2):
+                cols = slice(h * W // 2, (h + 1) * W // 2)
+                quantise(d_codes[g][:, cols], d_scales[g][:, cols], grouped["d", g][:, 2 * h * W:2 * (h + 1) * W])
 
         def copy_on(engine, dst, src):
             if engine == "scalar":
@@ -171,41 +208,56 @@ def tile_leontief_footprint_allocation_s3_kernel(
             grouped["r", c, g] = rot.tile([P, 4 * W], BF16, name="r_grouped", tag="grouped", align_bytes=64)
             dst = grouped["r", c, g][:]
             if c in PARKED:
-                interleave(engine, dst, r_raw[c, g][:])
+                interleave(engine, dst, loaded_req(c, g))
             else:
                 copy_on(
                     engine,
-                    dst.rearrange("p (t m j) -> p t m j", t=4, j=4),
-                    r_raw[c, g][:].rearrange("p j (m t) -> p t m j", t=4),
+                    dst.rearrange("p (t o i j) -> p o t i j", t=4, i=2, j=4),
+                    loaded_req(c, g).rearrange("p j (o i t) -> p o t i j", i=2, t=4),
                 )
 
+        def group_req_half(c, g, h):
+            if h == 1:
+                grouped["r", c, g] = rot.tile([P, 4 * W], BF16, name="r_grouped", tag="grouped", align_bytes=64)
+            interleave(
+                ("vector", "scalar")[h],
+                grouped["r", c, g][:, 2 * h * W:2 * (h + 1) * W],
+                loaded_req(c, g)[:, :, h * W // 2:(h + 1) * W // 2],
+            )
+
+        def quantise_req_half(c, g, h):
+            cols = slice(h * W // 2, (h + 1) * W // 2)
+            quantise(r_codes[c, g][:, cols], r_scales[c, g][:, cols], grouped["r", c, g][:, 2 * h * W:2 * (h + 1) * W])
+
         def quantise_req(c, g):
-            quantise(("r", c, g), r_codes[c, g], r_scales[c, g])
+            quantise(r_codes[c, g][:], r_scales[c, g][:], grouped["r", c, g][:])
 
         def group_emis(c, engine):
             grouped["e", c] = rot.tile([P, 4 * S], BF16, name="e_grouped", tag="grouped", align_bytes=64)
             interleave(engine, grouped["e", c][:], back[c][:] if c in PARKED else emis[c][:])
 
-        def quantise_emis(c):
-            quantise(("e", c), e_codes[c], e_scales[c])
+        def group_emis_shared(c):
+            grouped["e", c] = rot.tile([P, 4 * S], BF16, name="e_grouped", tag="grouped", align_bytes=64)
+            for h, engine in enumerate(("vector", "scalar")):
+                interleave(
+                    engine,
+                    grouped["e", c][:, 2 * h * S:2 * (h + 1) * S],
+                    back[c][:, :, h * S // 2:(h + 1) * S // 2],
+                )
 
-        def loaded_imp(c, g):
-            if c == 0:
-                return (w0a[:, 0, :], w0b[:, 0, :], w0c[:, 0, :], w0c[:, 1, :])[g], sc0[:, g, :]
-            if c == 1:
-                return w1[:, g, :], sc1[:, g, :]
-            return w23[:, g, (c - 2) * 2 * W:(c - 1) * 2 * W], sc23[:, g, (c - 2) * W:(c - 1) * W]
+        def quantise_emis(c):
+            quantise(e_codes[c][:], e_scales[c][:], grouped["e", c][:])
 
         def sort_words(c, g):
             nc.vector.tensor_copy(
-                out=w_sorted[c, g][:].rearrange("p (t m b) -> p t m b", t=4, b=2),
-                in_=loaded_imp(c, g)[0].rearrange("p (m t b) -> p t m b", t=4, b=2),
+                out=w_sorted[c, g][:].rearrange("p (t o i b) -> p o t i b", t=4, i=8, b=2),
+                in_=loaded_imp(c, g)[0].rearrange("p (o i t b) -> p o t i b", i=8, t=4, b=2),
             )
 
         def sort_scales(c, g):
             nc.vector.tensor_copy(
-                out=sc_sorted[c, g][:].rearrange("p (t m) -> p t m", t=4),
-                in_=loaded_imp(c, g)[1].rearrange("p (m t) -> p t m", t=4),
+                out=sc_sorted[c, g][:].rearrange("p (t o i) -> p o t i", t=4, i=16),
+                in_=loaded_imp(c, g)[1].rearrange("p (o i t) -> p o t i", i=16, t=4),
             )
 
         def sort_imp(c, g):
@@ -232,26 +284,24 @@ def tile_leontief_footprint_allocation_s3_kernel(
             nc.tensor.matmul_mx(
                 out=gross[c, j][:], lhsT=lhs, lhsT_scale=lhs_scale,
                 rhs=d_codes[g][:].bitcast(FP8X4), rhs_scale=d_scales[g][:],
-                start=(g == 0), stop=(g == GI + GD - 1),
+                start=(g == 0), stop=(g == G - 1),
             )
 
-        def imp_passes(c):
-            for g in range(GI):
-                for j in range(4):
-                    gross_pass(c, g, j)
+        def passes(c, g, tiles=range(4)):
+            for j in tiles:
+                gross_pass(c, g, j)
 
-        def emit(c, j):
+        def emit(c, j, cols=slice(0, S)):
             if c in PARKED:
                 col = 4 * c + j
-                gain, bias = vec_cols[:, 16 + col:17 + col], bias_cols[:, col:col + 1]
+                gain, bias = vec_cols[:, 8 + col:9 + col], bias_cols[:, col:col + 1]
             else:
-                gain, bias = gain_sorted[:, c // LAST, j:j + 1], bias_sorted[:, c // LAST, j:j + 1]
-            nc.scalar.activation(out=emis[c][:, j, :], in_=gross[c, j][:], func=IDENT, bias=bias, scale=gain)
+                gain, bias = gain_sorted[:, c - 2, j:j + 1], bias_sorted[:, c - 2, j:j + 1]
+            nc.scalar.activation(out=emis[c][:, j, cols], in_=gross[c, j][:, cols], func=IDENT, bias=bias, scale=gain)
 
-        def dom_passes(c):
-            for j in range(4):
-                for g in range(GI, GI + GD):
-                    gross_pass(c, g, j)
+        def close_tiles(c, tiles=range(4)):
+            for j in tiles:
+                gross_pass(c, G - 1, j)
                 emit(c, j)
 
         acc = {}
@@ -273,141 +323,154 @@ def tile_leontief_footprint_allocation_s3_kernel(
         def zero(plane):
             nc.vector.memset(plane[:].bitcast(I32), 0)
 
-        nc.sync.dma_start(out=d_imp[0][:], in_=dimp_v[:, :, 0:W])
+        for h in range(2):
+            nc.sync.dma_start(out=d_first[h][:], in_=dimp_v[:, 2 * h:2 * h + 2, 0:W])
+        nc.sync.dma_start(out=vec_rows[0:8, :], in_=exports[0:2 * W].rearrange("(j p) -> j p", p=P))
+        nc.sync.dma_start(out=vec_rows[8:16, :], in_=intensity[0:2 * W].rearrange("(j p) -> j p", p=P))
+        load_demand(1)
         zero(warm_in)
         zero(sc0)
-        nc.vector.quantize_mx(out=warm_codes[:].bitcast(FP8X4), scales=warm_scales[:], in_=warm_in[:])
-        zero(sc1)
-        zero(sc23)
+        quantise(warm_codes[:], warm_scales[:], warm_in[:])
+        zero(sc12)
+        zero(sc3)
         zero(a_scales)
         make_identity(nc, ident[:])
-        nc.scalar.activation(out=vec_f32[:], in_=ident[:], func=IDENT, scale=0.0)
+        nc.scalar.activation(out=vec_f32[:], in_=warm_in[:, 0:P], func=IDENT)
 
-        load_words(w0a, 0, 1, 0, 1)
-        nc.sync.dma_start(out=d_imp[1][:], in_=dimp_v[:, :, W:2 * W])
         load_scales(sc0, req_imp_scales, 0, W)
+        load_words(w0a, 0, 1, 0, 1)
+        load_demand(2)
         load_words(w0b, 1, 2, 0, 1)
-        nc.sync.dma_start(out=d_imp[2][:], in_=dimp_v[:, :, 2 * W:3 * W])
+        load_demand(3)
         load_words(w0c, 2, GI, 0, 1)
-        nc.sync.dma_start(out=d_imp[3][:], in_=dimp_v[:, :, 3 * W:4 * W])
-        nc.sync.dma_start(out=d_dom[:], in_=ddom_v)
-        nc.sync.dma_start(out=vec_rows[0:16, :], in_=exports.rearrange("(j p) -> j p", p=P))
-        nc.sync.dma_start(out=vec_rows[16:32, :], in_=intensity.rearrange("(j p) -> j p", p=P))
-        load_req(0, 0)
-        load_req(0, 1)
-        nc.sync.dma_start(out=exp_sorted[:], in_=exports.rearrange("(c p t) -> p c t", p=P, t=4)[:, 0:CH:LAST, :])
-        nc.sync.dma_start(out=int_sorted[:], in_=intensity.rearrange("(c p t) -> p c t", p=P, t=4)[:, 0:CH:LAST, :])
-        load_scales(sc1, req_imp_scales, W, W)
-        load_words(w1, 0, GI, 1, 2)
-        load_req(1, 0)
-        load_req(1, 1)
-        load_scales(sc23, req_imp_scales, 2 * W, 2 * W)
-        load_words(w23, 0, GI, 2, 4)
-        load_req(2, 0)
-        load_req(2, 1)
-        load_req(3, 0)
-        load_req(3, 1)
-
-        def quantise_demand(g):
-            quantise(("d", g), d_codes[g], d_scales[g])
-
-        def head_pass(g):
-            for j in range(4):
-                gross_pass(0, g, j)
+        load_demand(4)
+        load_demand(5)
+        load_scales(sc12, req_imp_scales, W, 2 * W)
+        load_words(w12[0], 0, 2, 1, 3)
+        load_words(w12[1], 2, GI, 1, 3)
+        load_req(0, 1, 0)
+        load_req(0, 1, 1)
+        load_req(1, 2, 0)
+        load_req(1, 2, 1)
+        load_req(2, CH, 0)
+        load_req(2, CH, 1)
+        nc.sync.dma_start(out=exp_sorted[:], in_=exports[2 * W:].rearrange("(c p t) -> p c t", p=P, t=4))
+        nc.sync.dma_start(out=int_sorted[:], in_=intensity[2 * W:].rearrange("(c p t) -> p c t", p=P, t=4))
+        load_scales(sc3, req_imp_scales, LAST * W, W)
+        load_words(w3, 0, GI, LAST, CH)
 
         warm_bank = bank(3, "warm_bank")
         warm(warm_bank, WARM_A)
+        presort_demand(0)
+        nc.vector.tensor_copy(out=vec_f32[0:16, :], in_=vec_rows[:])
         turn_demand(0)
-        warm(warm_bank, WARM_B)
-        sort_words(0, 0)
-        quantise_demand(0)
-        sort_scales(0, 0)
-        turn_demand(1)
-        head_pass(0)
-        sort_imp(0, 1)
-        quantise_demand(1)
-        turn_demand(2)
-        head_pass(1)
-        sort_imp(0, 2)
-        quantise_demand(2)
-        sort_imp(0, 3)
-        turn_demand(3)
-        head_pass(2)
-        quantise_demand(3)
-        nc.vector.tensor_copy(out=vec_f32[0:32, :], in_=vec_rows[:])
-        turn_demand(4)
-        head_pass(3)
-        group_req(0, 0, "vector")
-        quantise_demand(4)
-        quantise_req(0, 0)
-        turn_demand(5)
-        vec_bank = bank(4, "vec_bank")
+        vec_bank = bank(2, "vec_bank")
         nc.tensor.transpose(vec_bank[:, 0:P], vec_f32[:], ident[:])
-        nc.scalar.copy(out=vec_cols[:], in_=vec_bank[:, 0:32])
-        head_pass(4)
-        group_req(0, 1, "vector")
+        nc.scalar.copy(out=vec_cols[:], in_=vec_bank[:, 0:16])
+        warm(warm_bank, WARM_B)
+        presort_demand(1)
+        quantise_demand(0)
+        turn_demand(1)
+        warm(warm_bank, WARM_C)
+        passes(0, 0)
+        nc.vector.tensor_tensor(out=bias_cols[:], in0=vec_cols[:, 0:8], in1=vec_cols[:, 8:16], op=MULT)
+        for g in range(2, GI + 1):
+            presort_demand(g)
+            quantise_demand(g - 1)
+            turn_demand(g)
+            if g < GI:
+                passes(0, g - 1)
+        passes(0, 3, range(2))
+        presort_demand(5)
+        quantise_demand(4)
+        turn_demand(5)
+        passes(0, 3, range(2, 4))
         quantise_demand(5)
-        quantise_req(0, 1)
-        nc.vector.tensor_copy(out=gain_sorted[:], in_=int_sorted[:])
-        nc.vector.tensor_tensor(out=bias_sorted[:], in0=exp_sorted[:], in1=int_sorted[:], op=MULT)
-        nc.vector.tensor_tensor(out=bias_cols[:], in0=vec_cols[:, 0:16], in1=vec_cols[:, 16:32], op=MULT)
-        for j in range(4):
-            gross_pass(0, GI + GD - 1, j)
-            emit(0, j)
 
-        imp_passes(1)
-        group_emis(0, "scalar")
-        group_req(1, 0, "vector")
-        group_req(1, 1, "vector")
-        quantise_req(1, 0)
-        quantise_req(1, 1)
-        quantise_emis(0)
-        dom_passes(1)
-        store_emis(1, 0, 4)
+        for g in range(2):
+            passes(1, g, range(2))
+        for g in range(2):
+            passes(1, g, range(2, 4))
+        for g in range(2, GI):
+            passes(1, g)
+        sort_imp(2, 0)
+        sort_imp(2, 1)
+        blocks = [(c, g) for c in PARKED for g in range(GD)]
+        for c, g in blocks:
+            group_req_half(c, g, 1)
+        group_req_half(0, 0, 0)
+        sort_scales(2, 2)
+        quantise_req_half(0, 0, 0)
+        for (c, g), (c1, g1) in zip(blocks, blocks[1:]):
+            group_req_half(c1, g1, 0)
+            quantise_req_half(c, g, 1)
+            quantise_req_half(c1, g1, 0)
+        quantise_req_half(1, 1, 1)
+        for c in PARKED:
+            passes(c, GI)
+            close_tiles(c)
+        store_emis(0)
+        store_emis(1)
+        load_back(0)
+        load_back(1)
         load_scales(a_scales, alloc_scales, 0, H)
         nc.sync.dma_start(out=a_words[:].bitcast(I32), in_=alloc_words.bitcast(I32).rearrange("g p n -> p g n"))
-        load_back(1)
-
-        imp_passes(2)
-        sort_imp(3, 0)
-        sort_imp(3, 1)
-        group_req(2, 0, "vector")
-        group_req(2, 1, "scalar")
-        sort_imp(3, 2)
-        quantise_req(2, 0)
-        quantise_req(2, 1)
-        sort_imp(3, 3)
-        dom_passes(2)
-        store_emis(2, 0, 2)
-        store_emis(2, 2, 4)
-        load_back(2)
         nc.sync.dma_start(out=direct_rows[:], in_=direct.partition_broadcast(P))
 
-        imp_passes(3)
-        group_req(3, 0, "vector")
+        sort_words(2, 2)
+        sort_imp(2, 3)
+        for g in range(GI):
+            passes(2, g)
+        group_req(2, 0, "vector")
+        group_req(2, 1, "vector")
+        group_req(3, 0, "scalar")
         group_req(3, 1, "scalar")
-        group_emis(1, "vector")
-        quantise_req(3, 0)
-        quantise_emis(1)
-        quantise_req(3, 1)
-        dom_passes(3)
-        group_emis(2, "vector")
-        quantise_emis(2)
+        quantise_req(2, 0)
+        quantise_req(2, 1)
+        nc.vector.tensor_copy(out=gain_sorted[:], in_=int_sorted[:])
+        nc.vector.tensor_tensor(out=bias_sorted[:], in0=exp_sorted[:], in1=int_sorted[:], op=MULT)
+        passes(2, GI)
+        close_tiles(2)
 
-        half = S // 2
-        interleave("vector", e_half[0][:], emis[LAST][:, :, 0:half])
-        interleave("scalar", e_half[1][:], emis[LAST][:, :, half:S])
-        for h in range(2):
-            cols = slice(h * half, (h + 1) * half)
-            nc.vector.quantize_mx(
-                out=e_codes[LAST][:, cols].bitcast(FP8X4), scales=e_scales[LAST][:, cols], in_=e_half[h][:],
-            )
-        for c in range(2):
-            for a in range(4):
+        for g in range(GI):
+            sort_imp(3, g)
+            passes(3, g)
+        quantise_req(3, 0)
+        quantise_req(3, 1)
+        group_emis_shared(0)
+        group_emis(2, "vector")
+        group_emis_shared(1)
+        quantise_emis(0)
+        quantise_emis(2)
+        quantise_emis(1)
+        for j in range(4):
+            gross_pass(LAST, GI, j)
+            gross_pass(LAST, G - 1, j)
+            if j < 3:
+                emit(LAST, j)
+        emit(LAST, 3, slice(0, S // 2))
+        emit(LAST, 3, slice(S // 2, S))
+
+        def group_quarter(a, engine):
+            interleave(engine, e_quarter[a][:], emis[LAST][:, :, a * P:(a + 1) * P])
+
+        def quantise_quarter(a):
+            cols = slice(a * P, (a + 1) * P)
+            quantise(e_codes[LAST][:, cols], e_scales[LAST][:, cols], e_quarter[a][:])
+
+        group_quarter(0, "vector")
+        group_quarter(1, "vector")
+        group_quarter(3, "scalar")
+        quantise_quarter(0)
+        group_quarter(2, "vector")
+        for a in range(1, 4):
+            quantise_quarter(a)
+        for c in (0, 2, 1):
+            for a in range(3):
                 alloc_pass(c, a)
-        for pair in ((0, 1), (2, 3)):
-            for c in (2, 3):
-                for a in pair:
-                    alloc_pass(c, a)
-            for a in pair:
-                finish(a)
+        for a in range(3):
+            alloc_pass(LAST, a)
+            finish(a)
+        for c in range(CH):
+            alloc_pass(c, 3)
+        finish(3)

from contextlib import ExitStack

import concourse.mybir as mybir
from concourse.masks import make_identity

S, KD, KI, N, H = 512, 1024, 2048, 2048, 512
FLOPS = 2 * S * ((KD + KI) * N + N * H)

F32 = mybir.dt.float32
BF16 = mybir.dt.bfloat16
I32 = mybir.dt.int32
U32 = mybir.dt.uint32
U8 = mybir.dt.uint8
FP8X4 = mybir.dt.float8_e4m3fn_x4
FP4X4 = mybir.dt.float4_e2m1fn_x4
IDENT = mybir.ActivationFunctionType.Identity
ADD = mybir.AluOpType.add
MULT = mybir.AluOpType.mult

P = 128
W = 512
GI = KI // W
GD = KD // W
G = GI + GD
CH = N // W
LAST = CH - 1
PARKED = (0, 1)
SORTED = (2, 3)
WARM_A = 16
WARM_B = 6
WARM_C = 2


def tile_leontief_footprint_allocation_s3_kernel(
    tc, demand_dom, demand_imp, req_dom, req_imp_words, req_imp_scales,
    exports, intensity, alloc_words, alloc_scales, direct, out,
):
    nc = tc.nc
    with ExitStack() as ctx:
        keep = ctx.enter_context(tc.tile_pool(name="keep", bufs=1))
        rot = ctx.enter_context(tc.tile_pool(name="rot", bufs=5))
        psum = ctx.enter_context(tc.psum_pool(name="psum", bufs=1))
        ctx.enter_context(tc.manual_schedule())

        def kept(name, shape, dtype):
            return keep.tile(shape, dtype, name=name, align_bytes=64)

        def bank(b, name):
            return psum.tile([P, W], F32, name=name, tag="bank%d" % b)

        ident = kept("ident", [P, P], F32)
        warm_in = kept("warm_in", [P, W], BF16)
        warm_codes = kept("warm_codes", [P, P], U32)
        warm_scales = kept("warm_scales", [P, P], U8)
        d_first = [kept("d_first%d" % h, [P, 2, W], BF16) for h in range(2)]
        d_raw = {g: kept("d_raw%d" % g, [P, 4, W], BF16) for g in range(1, G)}
        d_codes = [kept("d_codes%d" % g, [P, W], U32) for g in range(G)]
        d_scales = [kept("d_scales%d" % g, [P, W], U8) for g in range(G)]
        w0a = kept("w0a", [P, 1, 2 * W], U8)
        w0b = kept("w0b", [P, 1, 2 * W], U8)
        w0c = kept("w0c", [P, 2, 2 * W], U8)
        w12 = [kept("w12_%d" % h, [P, 2, 4 * W], U8) for h in range(2)]
        w3 = kept("w3", [P, GI, 2 * W], U8)
        sc0 = kept("sc0", [P, GI, W], U8)
        sc12 = kept("sc12", [P, GI, 2 * W], U8)
        sc3 = kept("sc3", [P, GI, W], U8)
        w_sorted = {(c, g): kept("w_sorted%d_%d" % (c, g), [P, 2 * W], U8) for c in SORTED for g in range(GI)}
        sc_sorted = {(c, g): kept("sc_sorted%d_%d" % (c, g), [P, W], U8) for c in SORTED for g in range(GI)}
        a_words = kept("a_words", [P, CH, 2 * H], U8)
        a_scales = kept("a_scales", [P, CH, H], U8)
        r_raw = {
            (c, g): kept("r_raw%d_%d" % (c, g), [P, 4, n * W], BF16)
            for c, n in ((0, 1), (1, 1), (2, 2)) for g in range(GD)
        }
        r_codes = {(c, g): kept("r_codes%d_%d" % (c, g), [P, W], U32) for c in range(CH) for g in range(GD)}
        r_scales = {(c, g): kept("r_scales%d_%d" % (c, g), [P, W], U8) for c in range(CH) for g in range(GD)}
        vec_rows = kept("vec_rows", [16, P], BF16)
        vec_f32 = kept("vec_f32", [P, P], F32)
        vec_cols = kept("vec_cols", [P, 16], F32)
        bias_cols = kept("bias_cols", [P, 8], F32)
        exp_sorted = kept("exp_sorted", [P, 2, 4], BF16)
        int_sorted = kept("int_sorted", [P, 2, 4], BF16)
        gain_sorted = kept("gain_sorted", [P, 2, 4], F32)
        bias_sorted = kept("bias_sorted", [P, 2, 4], F32)
        direct_rows = kept("direct_rows", [P, H], BF16)
        emis = [kept("emis%d" % c, [P, 4, S], BF16) for c in range(CH)]
        back = {c: kept("back%d" % c, [P, 4, S], BF16) for c in PARKED}
        e_codes = [kept("e_codes%d" % c, [P, S], U32) for c in range(CH)]
        e_scales = [kept("e_scales%d" % c, [P, S], U8) for c in range(CH)]
        e_quarter = [kept("e_quarter%d" % a, [P, 4 * P], BF16) for a in range(4)]
        result = [kept("result%d" % a, [P, H], F32) for a in range(4)]

        words32 = req_imp_words.bitcast(I32).rearrange("g p n -> p g n")
        dimp_v = demand_imp.rearrange("(r a) k -> r a k", a=4)
        ddom_v = demand_dom.rearrange("(r a) k -> r a k", a=4)
        park = out.bitcast(BF16).rearrange("a (b w) -> (a b) w", b=2)
        out_v = out.rearrange("(r a) h -> r a h", a=4)

        def load_scales(plane, src, col0, cols):
            src32 = src.bitcast(I32)
            for r in range(4):
                nc.sync.dma_start(
                    out=plane[r:P:32, :, :].bitcast(I32),
                    in_=src32[:, r:16:4, col0 // 4:(col0 + cols) // 4].rearrange("g q n -> q g n"),
                )

        def load_words(dst, g0, g1, c0, c1):
            nc.sync.dma_start(out=dst[:].bitcast(I32), in_=words32[:, g0:g1, c0 * W // 2:c1 * W // 2])

        def load_demand(g):
            if g < GI:
                src = dimp_v[:, :, g * W:(g + 1) * W]
            else:
                src = ddom_v[:, :, (g - GI) * W:(g - GI + 1) * W]
            nc.sync.dma_start(out=d_raw[g][:], in_=src)

        def load_req(c0, c1, g):
            nc.sync.dma_start(
                out=r_raw[c0, g][:],
                in_=req_dom[g * W:(g + 1) * W, c0 * W:c1 * W].rearrange("(p j) n -> p j n", j=4),
            )

        def loaded_req(c, g):
            if c == LAST:
                return r_raw[2, g][:, :, W:2 * W]
            return r_raw[c, g][:, :, 0:W]

        def loaded_imp(c, g):
            if c == 0:
                return (w0a[:, 0, :], w0b[:, 0, :], w0c[:, 0, :], w0c[:, 1, :])[g], sc0[:, g, :]
            if c == LAST:
                return w3[:, g, :], sc3[:, g, :]
            return w12[g // 2][:, g % 2, (c - 1) * 2 * W:c * 2 * W], sc12[:, g, (c - 1) * W:c * W]

        def parked(c):
            return park[c * W:(c + 1) * W, :]

        def store_emis(c):
            nc.sync.dma_start(out=parked(c).rearrange("(j p) w -> p j w", p=P), in_=emis[c][:])

        def load_back(c):
            nc.sync.dma_start(out=back[c][:], in_=parked(c).rearrange("(p t) w -> p t w", t=4))

        def warm(dst, n):
            for i in range(n):
                nc.tensor.matmul_mx(
                    out=dst[:, 0:P], lhsT=warm_codes[:].bitcast(FP8X4), lhsT_scale=warm_scales[:],
                    rhs=warm_codes[:].bitcast(FP8X4), rhs_scale=warm_scales[:], start=(i == 0), stop=(i == n - 1),
                )

        grouped = {}
        presorted = {}

        def presort(g, h):
            if g == 0:
                words = d_first[h][:].bitcast(F32)
            else:
                words = d_raw[g][:].bitcast(F32)[:, 2 * h:2 * h + 2, :]
            presorted[g, h] = rot.tile([P, 2, 2, P], F32, name="presorted", tag="presorted", bufs=4, align_bytes=64)
            nc.vector.tensor_copy(
                out=presorted[g, h][:].rearrange("p u a (o i) -> p (a o) u i", i=4),
                in_=words.rearrange("p a (o i u) -> p (a o) u i", i=4, u=2),
            )

        def presort_demand(g):
            for h in range(2):
                presort(g, h)

        def turn_half(g, h):
            if h == 0:
                grouped["d", g] = rot.tile([P, 4 * W], BF16, name="d_grouped", tag="grouped", align_bytes=64)
            xt = bank(4 + 2 * (g % 2) + h, "xt")
            for a in range(2):
                for u in range(2):
                    q = 2 * a + u
                    nc.tensor.transpose(xt[:, q * P:(q + 1) * P], presorted[g, h][:, u, a, :], ident[:])
            nc.scalar.copy(
                out=grouped["d", g][:].bitcast(F32)[:, h * W:(h + 1) * W].rearrange("p (a r u) -> p a r u", a=2, u=2),
                in_=xt[:].rearrange("p (a u r) -> p a r u", a=2, u=2),
            )

        def turn_demand(g):
            for h in range(2):
                turn_half(g, h)

        def quantise(codes, scales, values):
            nc.vector.quantize_mx(out=codes.bitcast(FP8X4), scales=scales, in_=values)

        def quantise_demand(g):
            for h in range(2):
                cols = slice(h * W // 2, (h + 1) * W // 2)
                quantise(d_codes[g][:, cols], d_scales[g][:, cols], grouped["d", g][:, 2 * h * W:2 * (h + 1) * W])

        def copy_on(engine, dst, src):
            if engine == "scalar":
                nc.scalar.copy(out=dst, in_=src)
            else:
                nc.vector.tensor_copy(out=dst, in_=src)

        def interleave(engine, dst, src):
            copy_on(
                engine,
                dst.rearrange("p (c i t) -> p c t i", i=4, t=4),
                src.rearrange("p t (c i) -> p c t i", i=4),
            )

        def group_req(c, g, engine):
            grouped["r", c, g] = rot.tile([P, 4 * W], BF16, name="r_grouped", tag="grouped", align_bytes=64)
            dst = grouped["r", c, g][:]
            if c in PARKED:
                interleave(engine, dst, loaded_req(c, g))
            else:
                copy_on(
                    engine,
                    dst.rearrange("p (t o i j) -> p o t i j", t=4, i=2, j=4),
                    loaded_req(c, g).rearrange("p j (o i t) -> p o t i j", i=2, t=4),
                )

        def group_req_half(c, g, h):
            if h == 1:
                grouped["r", c, g] = rot.tile([P, 4 * W], BF16, name="r_grouped", tag="grouped", align_bytes=64)
            interleave(
                ("vector", "scalar")[h],
                grouped["r", c, g][:, 2 * h * W:2 * (h + 1) * W],
                loaded_req(c, g)[:, :, h * W // 2:(h + 1) * W // 2],
            )

        def quantise_req_half(c, g, h):
            cols = slice(h * W // 2, (h + 1) * W // 2)
            quantise(r_codes[c, g][:, cols], r_scales[c, g][:, cols], grouped["r", c, g][:, 2 * h * W:2 * (h + 1) * W])

        def quantise_req(c, g):
            quantise(r_codes[c, g][:], r_scales[c, g][:], grouped["r", c, g][:])

        def group_emis(c, engine):
            grouped["e", c] = rot.tile([P, 4 * S], BF16, name="e_grouped", tag="grouped", align_bytes=64)
            interleave(engine, grouped["e", c][:], back[c][:] if c in PARKED else emis[c][:])

        def group_emis_shared(c):
            grouped["e", c] = rot.tile([P, 4 * S], BF16, name="e_grouped", tag="grouped", align_bytes=64)
            for h, engine in enumerate(("vector", "scalar")):
                interleave(
                    engine,
                    grouped["e", c][:, 2 * h * S:2 * (h + 1) * S],
                    back[c][:, :, h * S // 2:(h + 1) * S // 2],
                )

        def quantise_emis(c):
            quantise(e_codes[c][:], e_scales[c][:], grouped["e", c][:])

        def sort_words(c, g):
            nc.vector.tensor_copy(
                out=w_sorted[c, g][:].rearrange("p (t o i b) -> p o t i b", t=4, i=8, b=2),
                in_=loaded_imp(c, g)[0].rearrange("p (o i t b) -> p o t i b", i=8, t=4, b=2),
            )

        def sort_scales(c, g):
            nc.vector.tensor_copy(
                out=sc_sorted[c, g][:].rearrange("p (t o i) -> p o t i", t=4, i=16),
                in_=loaded_imp(c, g)[1].rearrange("p (o i t) -> p o t i", i=16, t=4),
            )

        def sort_imp(c, g):
            sort_words(c, g)
            sort_scales(c, g)

        def imp_operand(c, g, j):
            if c in SORTED:
                wt, st = w_sorted[c, g][:], sc_sorted[c, g][:]
            else:
                wt, st = loaded_imp(c, g)
            return wt[:, 2 * j * P:2 * (j + 1) * P].bitcast(FP4X4), st[:, j * P:(j + 1) * P]

        gross = {}

        def gross_pass(c, g, j):
            if g == 0:
                gross[c, j] = bank(4 * (c % 2) + j, "gross")
            if g < GI:
                lhs, lhs_scale = imp_operand(c, g, j)
            else:
                cols = slice(j * P, (j + 1) * P)
                lhs, lhs_scale = r_codes[c, g - GI][:, cols].bitcast(FP8X4), r_scales[c, g - GI][:, cols]
            nc.tensor.matmul_mx(
                out=gross[c, j][:], lhsT=lhs, lhsT_scale=lhs_scale,
                rhs=d_codes[g][:].bitcast(FP8X4), rhs_scale=d_scales[g][:],
                start=(g == 0), stop=(g == G - 1),
            )

        def passes(c, g, tiles=range(4)):
            for j in tiles:
                gross_pass(c, g, j)

        def emit(c, j, cols=slice(0, S)):
            if c in PARKED:
                col = 4 * c + j
                gain, bias = vec_cols[:, 8 + col:9 + col], bias_cols[:, col:col + 1]
            else:
                gain, bias = gain_sorted[:, c - 2, j:j + 1], bias_sorted[:, c - 2, j:j + 1]
            nc.scalar.activation(out=emis[c][:, j, cols], in_=gross[c, j][:, cols], func=IDENT, bias=bias, scale=gain)

        def close_tiles(c, tiles=range(4)):
            for j in tiles:
                gross_pass(c, G - 1, j)
                emit(c, j)

        acc = {}

        def alloc_pass(c, a):
            if c == 0:
                acc[a] = bank(a, "acc")
            cols = slice(a * P, (a + 1) * P)
            nc.tensor.matmul_mx(
                out=acc[a][:], lhsT=e_codes[c][:, cols].bitcast(FP8X4), lhsT_scale=e_scales[c][:, cols],
                rhs=a_words[:, c, :].bitcast(FP4X4), rhs_scale=a_scales[:, c, :],
                start=(c == 0), stop=(c == LAST),
            )

        def finish(a):
            nc.vector.tensor_tensor(out=result[a][:], in0=acc[a][:], in1=direct_rows[:], op=ADD)
            nc.sync.dma_start(out=out_v[:, a, :], in_=result[a][:])

        def zero(plane):
            nc.vector.memset(plane[:].bitcast(I32), 0)

        for h in range(2):
            nc.sync.dma_start(out=d_first[h][:], in_=dimp_v[:, 2 * h:2 * h + 2, 0:W])
        nc.sync.dma_start(out=vec_rows[0:8, :], in_=exports[0:2 * W].rearrange("(j p) -> j p", p=P))
        nc.sync.dma_start(out=vec_rows[8:16, :], in_=intensity[0:2 * W].rearrange("(j p) -> j p", p=P))
        load_demand(1)
        zero(warm_in)
        zero(sc0)
        quantise(warm_codes[:], warm_scales[:], warm_in[:])
        zero(sc12)
        zero(sc3)
        zero(a_scales)
        make_identity(nc, ident[:])
        nc.scalar.activation(out=vec_f32[:], in_=warm_in[:, 0:P], func=IDENT)

        load_scales(sc0, req_imp_scales, 0, W)
        load_words(w0a, 0, 1, 0, 1)
        load_demand(2)
        load_words(w0b, 1, 2, 0, 1)
        load_demand(3)
        load_words(w0c, 2, GI, 0, 1)
        load_demand(4)
        load_demand(5)
        load_scales(sc12, req_imp_scales, W, 2 * W)
        load_words(w12[0], 0, 2, 1, 3)
        load_words(w12[1], 2, GI, 1, 3)
        load_req(0, 1, 0)
        load_req(0, 1, 1)
        load_req(1, 2, 0)
        load_req(1, 2, 1)
        load_req(2, CH, 0)
        load_req(2, CH, 1)
        nc.sync.dma_start(out=exp_sorted[:], in_=exports[2 * W:].rearrange("(c p t) -> p c t", p=P, t=4))
        nc.sync.dma_start(out=int_sorted[:], in_=intensity[2 * W:].rearrange("(c p t) -> p c t", p=P, t=4))
        load_scales(sc3, req_imp_scales, LAST * W, W)
        load_words(w3, 0, GI, LAST, CH)

        warm_bank = bank(3, "warm_bank")
        warm(warm_bank, WARM_A)
        presort_demand(0)
        nc.vector.tensor_copy(out=vec_f32[0:16, :], in_=vec_rows[:])
        turn_demand(0)
        vec_bank = bank(2, "vec_bank")
        nc.tensor.transpose(vec_bank[:, 0:P], vec_f32[:], ident[:])
        nc.scalar.copy(out=vec_cols[:], in_=vec_bank[:, 0:16])
        warm(warm_bank, WARM_B)
        presort_demand(1)
        quantise_demand(0)
        turn_demand(1)
        warm(warm_bank, WARM_C)
        passes(0, 0)
        nc.vector.tensor_tensor(out=bias_cols[:], in0=vec_cols[:, 0:8], in1=vec_cols[:, 8:16], op=MULT)
        for g in range(2, GI + 1):
            presort_demand(g)
            quantise_demand(g - 1)
            turn_demand(g)
            if g < GI:
                passes(0, g - 1)
        passes(0, 3, range(2))
        presort_demand(5)
        quantise_demand(4)
        turn_demand(5)
        passes(0, 3, range(2, 4))
        quantise_demand(5)

        for g in range(2):
            passes(1, g, range(2))
        for g in range(2):
            passes(1, g, range(2, 4))
        for g in range(2, GI):
            passes(1, g)
        sort_imp(2, 0)
        sort_imp(2, 1)
        blocks = [(c, g) for c in PARKED for g in range(GD)]
        for c, g in blocks:
            group_req_half(c, g, 1)
        group_req_half(0, 0, 0)
        sort_scales(2, 2)
        quantise_req_half(0, 0, 0)
        for (c, g), (c1, g1) in zip(blocks, blocks[1:]):
            group_req_half(c1, g1, 0)
            quantise_req_half(c, g, 1)
            quantise_req_half(c1, g1, 0)
        quantise_req_half(1, 1, 1)
        for c in PARKED:
            passes(c, GI)
            close_tiles(c)
        store_emis(0)
        store_emis(1)
        load_back(0)
        load_back(1)
        load_scales(a_scales, alloc_scales, 0, H)
        nc.sync.dma_start(out=a_words[:].bitcast(I32), in_=alloc_words.bitcast(I32).rearrange("g p n -> p g n"))
        nc.sync.dma_start(out=direct_rows[:], in_=direct.partition_broadcast(P))

        sort_words(2, 2)
        sort_imp(2, 3)
        for g in range(GI):
            passes(2, g)
        group_req(2, 0, "vector")
        group_req(2, 1, "vector")
        group_req(3, 0, "scalar")
        group_req(3, 1, "scalar")
        quantise_req(2, 0)
        quantise_req(2, 1)
        nc.vector.tensor_copy(out=gain_sorted[:], in_=int_sorted[:])
        nc.vector.tensor_tensor(out=bias_sorted[:], in0=exp_sorted[:], in1=int_sorted[:], op=MULT)
        passes(2, GI)
        close_tiles(2)

        for g in range(GI):
            sort_imp(3, g)
            passes(3, g)
        quantise_req(3, 0)
        quantise_req(3, 1)
        group_emis_shared(0)
        group_emis(2, "vector")
        group_emis_shared(1)
        quantise_emis(0)
        quantise_emis(2)
        quantise_emis(1)
        for j in range(4):
            gross_pass(LAST, GI, j)
            gross_pass(LAST, G - 1, j)
            if j < 3:
                emit(LAST, j)
        emit(LAST, 3, slice(0, S // 2))
        emit(LAST, 3, slice(S // 2, S))

        def group_quarter(a, engine):
            interleave(engine, e_quarter[a][:], emis[LAST][:, :, a * P:(a + 1) * P])

        def quantise_quarter(a):
            cols = slice(a * P, (a + 1) * P)
            quantise(e_codes[LAST][:, cols], e_scales[LAST][:, cols], e_quarter[a][:])

        group_quarter(0, "vector")
        group_quarter(1, "vector")
        group_quarter(3, "scalar")
        quantise_quarter(0)
        group_quarter(2, "vector")
        for a in range(1, 4):
            quantise_quarter(a)
        for c in (0, 2, 1):
            for a in range(3):
                alloc_pass(c, a)
        for a in range(3):
            alloc_pass(LAST, a)
            finish(a)
        for c in range(CH):
            alloc_pass(c, 3)
        finish(3)
